import numpy as np
import ml_dtypes


def mxq(x, axis, fmt="e4m3"):
    dtype, down = {"e4m3": (ml_dtypes.float8_e4m3fn, 7), "e5m2": (ml_dtypes.float8_e5m2, 14)}[fmt]
    v = np.moveaxis(np.asarray(x, np.float32).astype(ml_dtypes.bfloat16).astype(np.float64), axis, -1)
    blocks = v.reshape(v.shape[:-1] + (-1, 32))
    amax = np.abs(blocks).max(-1, keepdims=True)
    byte = np.maximum(np.where(amax > 0, np.frexp(amax)[1] - 1 + 127, 0) - down, 1)
    scale = np.exp2(byte - 127.0)
    codes = (blocks / scale).astype(np.float32).astype(dtype).astype(np.float64)
    return np.moveaxis((codes * scale).reshape(v.shape), -1, axis)


WIDE = False


def mx_kscale(k):
    if not WIDE:
        return np.ones(k)
    levels = np.array([24, -24, 12, -12, 0])
    if k % 512:
        return np.exp2(np.random.permutation(np.resize(levels, k // 32))).repeat(32)
    a = np.empty((k // 512, 16))
    for p in range(k // 512):
        a[p, :8] = np.random.permutation(np.resize(levels, 8))
        for g in range(8):
            far = levels[np.abs(levels - a[p, g]) >= 10]
            a[p, g + 8] = far[np.random.randint(len(far))]
    return np.exp2(a.ravel()).repeat(32)


def f64(x):
    return np.asarray(x).astype(np.float64)


def striped(idx):
    return np.tile(idx.reshape(-1, 16).T, (8, 1)).astype(np.uint16)


def unstriped(offs):
    return offs[:16].T.reshape(-1).astype(np.int64)


E2M1 = np.array([0.0, 0.5, 1.0, 1.5, 2.0, 3.0, 4.0, 6.0, -0.0, -0.5, -1.0, -1.5, -2.0, -3.0, -4.0, -6.0])


def pack_weight(w, fmt):
    k, n = w.shape
    w = f64(np.asarray(w, np.float32).astype(ml_dtypes.bfloat16)).reshape(k // 32, 32, n)
    amax = np.abs(w).max(1)
    if fmt == "e4m3":
        byte = np.frexp(amax)[1] - 1 + 127 - 7
    else:
        mant, ex = np.frexp(amax / 6.0)
        byte = np.where(mant > 0.5, ex, ex - 1) + 127
    byte = np.clip(np.where(amax > 0, byte, 1), 1, 254)
    scaled = (w * np.exp2(127.0 - byte)[:, None, :]).reshape(k, n).astype(np.float32)
    by_word = np.ascontiguousarray(scaled.reshape(k // 512, 128, 4, n).transpose(0, 1, 3, 2))
    if fmt == "e4m3":
        words = by_word.astype(ml_dtypes.float8_e4m3fn).view(np.uint8)
    else:
        c = by_word.astype(ml_dtypes.float4_e2m1fn).view(np.uint8) & 0xF
        words = (c[..., 0::2] | (c[..., 1::2] << 4)).reshape(k // 512, 128, 2 * n)
    return np.ascontiguousarray(words), np.ascontiguousarray(byte.astype(np.uint8).reshape(k // 512, 16, n))


def unpack_weight(words, scales, fmt):
    g, _, n = scales.shape
    words = np.ascontiguousarray(words).reshape(g, 128, n, -1)
    if fmt == "e4m3":
        vals = words.view(ml_dtypes.float8_e4m3fn).astype(np.float64)
    else:
        nib = np.empty((g, 128, n, 4), np.uint8)
        nib[..., 0::2] = words & 0xF
        nib[..., 1::2] = words >> 4
        vals = E2M1[nib]
    vals = vals * np.repeat(np.exp2(scales.astype(np.float64) - 127.0), 8, axis=1)[..., None]
    return vals.transpose(0, 1, 3, 2).reshape(g * 512, n)


def planes(y):
    n, m = y.shape
    v = y.astype(np.float32).astype(ml_dtypes.bfloat16).astype(np.float64).reshape(n // 32, 32, m)
    top = np.abs(v).max(1)
    byte = np.clip(np.where(top > 0, np.frexp(top)[1] - 1 + 127 - 7, 1), 1, 254)
    codes = (v * np.exp2(127.0 - byte)[:, None, :]).reshape(n, m).astype(np.float32).astype(ml_dtypes.float8_e4m3fn).view(np.uint8)
    words = codes.reshape(n // 512, 128, 4, m).transpose(0, 1, 3, 2)
    return np.ascontiguousarray(words), np.ascontiguousarray(byte.astype(np.uint8).reshape(n // 512, 16, m))


def silu(f):
    return f / (1.0 + np.exp(-np.maximum(f, -700.0)))


def sigm(f):
    return 1.0 / (1.0 + np.exp(-np.maximum(f, -700.0)))


K, N, T, J = 512, 512, 4096, 1024


def setup_inputs():
    n = np.random.standard_normal
    s = mx_kscale(K)[:, None]
    p_tab = pack_weight(n((K, T)) * s, "e4m3")
    p_wg = pack_weight(n((K, N)) / np.sqrt(K) / s, "e2m1")
    p_wh4 = pack_weight(n((K, N)) / np.sqrt(K) / s, "e2m1")
    return {
        "tab_words": p_tab[0],
        "tab_scales": p_tab[1],
        "wg_words": p_wg[0],
        "wg_scales": p_wg[1],
        "wh4_words": p_wh4[0],
        "wh4_scales": p_wh4[1],
        "whd": (0.4 * (n((K, N)) / np.sqrt(K) / s)).astype(np.float32),
        "bg": (0.3 * n(N) - 1.0).astype(np.float32),
        "rT": (n((N, T))).astype(np.float32),
        "offs": striped(np.random.permutation(T)[:J]),
    }


def reference(tab_words, tab_scales, wg_words, wg_scales, wh4_words, wh4_scales, whd, bg, rT, offs):
    idx = unstriped(offs)
    tab_ = unpack_weight(tab_words, tab_scales, "e4m3")[:, idx]
    wg_ = unpack_weight(wg_words, wg_scales, "e2m1")
    wh4_ = unpack_weight(wh4_words, wh4_scales, "e2m1")
    whd_ = mxq(f64(whd), 0, "e4m3")
    ga = wg_.T @ tab_
    gate = sigm(ga + f64(bg)[:, None])
    ha = wh4_.T @ tab_ + whd_.T @ tab_
    out_0 = f64(rT)[:, idx] + gate * (silu(ha) - f64(rT)[:, idx])
    return (out_0,) + planes(out_0)

@@ -1,0 +1,174 @@
+from contextlib import ExitStack
+
+import concourse.mybir as mybir
+
+K, N, T, J = 512, 512, 4096, 1024
+FLOPS = 3 * 2 * K * N * J
+
+F32 = mybir.dt.float32
+BF16 = mybir.dt.bfloat16
+I32 = mybir.dt.int32
+U32 = mybir.dt.uint32
+U16 = mybir.dt.uint16
+U8 = mybir.dt.uint8
+FP8X4 = mybir.dt.float8_e4m3fn_x4
+FP4X4 = mybir.dt.float4_e2m1fn_x4
+ACT = mybir.ActivationFunctionType
+ALU = mybir.AluOpType
+
+P = 128
+PACK = 4
+HALF = 512
+CHUNK = 256
+PER_COL = 16
+
+
+def tile_list_hwayt_dl_siluP_kernel(
+    tc, tab_words, tab_scales, wg_words, wg_scales, wh4_words, wh4_scales, whd, bg, rT, offs, out_0, out_1, out_2
+):
+    nc = tc.nc
+    halves = J // HALF
+    with ExitStack() as ctx:
+        keep = ctx.enter_context(tc.tile_pool(name="keep", bufs=1))
+        big = ctx.enter_context(tc.tile_pool(name="big", bufs=3))
+        work = ctx.enter_context(tc.tile_pool(name="work", bufs=8))
+        psum = ctx.enter_context(tc.psum_pool(name="psum", bufs=8))
+
+        offsets = keep.tile([P, J // PER_COL], U16, name="offsets")
+        nc.sync.dma_start(offsets[:], offs)
+
+        def picked(window, j0, j1):
+            return window[:].indirect(offsets[:, j0 // PER_COL : j1 // PER_COL])
+
+        whd_raw = big.tile([P, PACK, N], F32, tag="big", name="whd_raw", align_bytes=64)
+        nc.sync.dma_start(whd_raw[:], whd.rearrange("(p i) n -> p i n", i=PACK))
+
+        w4_raw = [keep.tile([P, N], U16, name="w4_raw%d" % w, align_bytes=64) for w in range(2)]
+        for w, src in enumerate((wh4_words, wg_words)):
+            nc.sync.dma_start(w4_raw[w][:].bitcast(I32), src[0].bitcast(I32))
+
+        tabw = big.tile([P, T], U32, tag="big", name="tabw", align_bytes=64)
+        nc.sync.dma_start(tabw[:].bitcast(I32), tab_words[0].rearrange("p t i -> p (t i)").bitcast(I32))
+
+        r_rows = rT.rearrange("(p i) t -> p i t", i=PACK)
+        r_tiles = []
+
+        def load_r(i):
+            r_i = big.tile([P, T], F32, tag="big", name="r%d" % i, align_bytes=64)
+            nc.sync.dma_start(r_i[:], r_rows[:, i, :])
+            r_tiles.append(r_i)
+
+        load_r(0)
+
+        bias_raw = keep.tile([P, PACK], F32, name="bias_raw")
+        nc.scalar.dma_start(bias_raw[:], bg.rearrange("(p i) -> p i", i=PACK))
+
+        tabs = keep.tile([P, T], U8, name="tabs", align_bytes=64)
+        nc.vector.memset(tabs[:].bitcast(I32), 0)
+        nc.scalar.dma_start(tabs[0:P:8, :].bitcast(I32), tab_scales[0].bitcast(I32))
+
+        s4_raw = [keep.tile([P, N], U8, name="s4_raw%d" % w, align_bytes=64) for w in range(2)]
+        for w, src in enumerate((wh4_scales, wg_scales)):
+            nc.gpsimd.memset(s4_raw[w][:].bitcast(I32), 0)
+        for w, src in enumerate((wh4_scales, wg_scales)):
+            for q in range(4):
+                nc.gpsimd.dma_start(
+                    s4_raw[w][32 * q : 32 * q + 4, :].bitcast(I32), src[0, 4 * q : 4 * q + 4, :].bitcast(I32)
+                )
+
+        v_scales = keep.tile([P, J], U8, name="v_scales", align_bytes=64)
+        nc.vector.memset(v_scales[:].bitcast(I32), 0)
+        gathered_scales = keep.tile([P, J], U8, name="gathered_scales", align_bytes=64)
+        nc.vector.tensor_copy(gathered_scales[:], picked(tabs, 0, J))
+        for r in range(4):
+            nc.scalar.dma_start(v_scales[r:P:32, :].bitcast(I32), gathered_scales[8 * r : P : 32, :].bitcast(I32))
+
+        half_bias = keep.tile([P, PACK], F32, name="half_bias")
+        nc.vector.tensor_scalar_mul(half_bias[:], bias_raw[:], 0.5)
+
+        whd_bf = keep.tile([P, PACK, P, PACK], BF16, name="whd_bf", align_bytes=64)
+        nc.scalar.copy(
+            whd_bf[:].rearrange("p i m e -> p m e i"),
+            whd_raw[:].rearrange("p e (m i) -> p m e i", i=PACK),
+        )
+        load_r(1)
+        whd_codes = keep.tile([P, N], U32, name="whd_codes", align_bytes=64)
+        whd_scales = keep.tile([P, N], U8, name="whd_scales", align_bytes=64)
+        nc.vector.quantize_mx(
+            out=whd_codes[:].bitcast(FP8X4), scales=whd_scales[:], in_=whd_bf[:].rearrange("p i m e -> p (i m e)")
+        )
+
+        w4 = [keep.tile([P, N], U16, name="w4_%d" % w, align_bytes=64) for w in range(2)]
+        s4 = [keep.tile([P, N], U8, name="s4_%d" % w, align_bytes=64) for w in range(2)]
+        for w in range(2):
+            nc.scalar.copy(
+                w4[w][:].rearrange("p (i m) -> p m i", i=PACK), w4_raw[w][:].rearrange("p (m i) -> p m i", i=PACK)
+            )
+            nc.vector.tensor_copy(
+                s4[w][:].rearrange("p (i m) -> p m i", i=PACK), s4_raw[w][:].rearrange("p (m i) -> p m i", i=PACK)
+            )
+
+        v_words = []
+        for h in range(halves):
+            words_h = keep.tile([P, HALF], U32, name="v_words%d" % h, align_bytes=64)
+            nc.vector.tensor_copy(words_h[:], picked(tabw, h * HALF, (h + 1) * HALF))
+            v_words.append(words_h)
+        load_r(2)
+
+        y = keep.tile([P, PACK, J], F32, name="y", align_bytes=64)
+        y_bf = keep.tile([P, J * PACK], BF16, name="y_bf", align_bytes=64)
+        y_codes = keep.tile([P, J], U32, name="y_codes", align_bytes=64)
+        y_scales = keep.tile([P, J], U8, name="y_scales", align_bytes=64)
+        out_rows = out_0.rearrange("(p i) j -> p i j", i=PACK)
+        out_words = out_1[0].rearrange("p j i -> p (j i)").bitcast(I32)
+
+        for i in range(PACK):
+            cols = slice(i * P, (i + 1) * P)
+            made, keep_share = [], []
+            for h in range(halves):
+                js = slice(h * HALF, (h + 1) * HALF)
+                rhs = v_words[h][:].bitcast(FP8X4)
+                ha = psum.tile([P, HALF], F32, tag="acc", name="ha")
+                nc.tensor.matmul_mx(ha[:], w4[0][:, cols].bitcast(FP4X4), s4[0][:, cols], rhs, v_scales[:, js],
+                                    start=True, stop=False)
+                nc.tensor.matmul_mx(ha[:], whd_codes[:, cols].bitcast(FP8X4), whd_scales[:, cols], rhs,
+                                    v_scales[:, js], start=False, stop=True)
+                ga = psum.tile([P, HALF], F32, tag="acc", name="ga")
+                nc.tensor.matmul_mx(ga[:], w4[1][:, cols].bitcast(FP4X4), s4[1][:, cols], rhs, v_scales[:, js],
+                                    start=True, stop=True)
+                s = work.tile([P, HALF], F32, name="s")
+                nc.scalar.activation(s[:], ha[:], ACT.Silu)
+                th = work.tile([P, HALF], F32, name="th")
+                nc.scalar.activation(th[:], ga[:], ACT.Tanh, bias=half_bias[:, i : i + 1], scale=0.5)
+                u = work.tile([P, HALF], F32, name="u")
+                nc.scalar.activation(u[:], th[:], ACT.Copy, bias=0.5, scale=-0.5)
+                gs2 = work.tile([P, HALF], F32, name="gs2")
+                nc.vector.scalar_tensor_tensor(gs2[:], th[:], 1.0, s[:], ALU.add, ALU.mult)
+                made.append(gs2)
+                keep_share.append(u)
+            step = HALF if i < PACK - 1 else CHUNK
+            for j0 in range(0, J, step):
+                h, o = divmod(j0, HALF)
+                ru = work.tile([P, step], F32, name="ru")
+                nc.vector.tensor_tensor(ru[:], picked(r_tiles[i], j0, j0 + step), keep_share[h][:, o : o + step], ALU.mult)
+                nc.vector.scalar_tensor_tensor(
+                    y[:, i, j0 : j0 + step], made[h][:, o : o + step], 0.5, ru[:], ALU.mult, ALU.add
+                )
+                if i == PACK - 1:
+                    nc.sync.dma_start(out_rows[:, i, j0 : j0 + step], y[:, i, j0 : j0 + step])
+                    bf = y_bf[:, PACK * j0 : PACK * (j0 + step)]
+                    nc.scalar.copy(
+                        bf.rearrange("p (c a i) -> p c i a", a=4, i=PACK),
+                        y[:, :, j0 : j0 + step].rearrange("p i (c a) -> p c i a", a=4),
+                    )
+                    nc.vector.quantize_mx(
+                        out=y_codes[:, j0 : j0 + step].bitcast(FP8X4), scales=y_scales[:, j0 : j0 + step], in_=bf
+                    )
+                    nc.sync.dma_start(out_words[:, j0 : j0 + step], y_codes[:, j0 : j0 + step].bitcast(I32))
+            if i == 0:
+                load_r(3)
+            if i < PACK - 1:
+                nc.sync.dma_start(out_rows[:, i, :], y[:, i, :])
+        for q in range(4):
+            eng = nc.scalar if q % 2 else nc.sync
+            eng.dma_start(out_2[0, 4 * q : 4 * q + 4, :].bitcast(I32), y_scales[32 * q : 32 * q + 4, :].bitcast(I32))

@@ -21,6 +21,7 @@ PACK = 4
 HALF = 512
 CHUNK = 256
 PER_COL = 16
+ROW0 = 16
 
 
 def tile_list_hwayt_dl_siluP_kernel(
@@ -30,7 +31,7 @@ def tile_list_hwayt_dl_siluP_kernel(
     halves = J // HALF
     with ExitStack() as ctx:
         keep = ctx.enter_context(tc.tile_pool(name="keep", bufs=1))
-        big = ctx.enter_context(tc.tile_pool(name="big", bufs=3))
+        big = ctx.enter_context(tc.tile_pool(name="big", bufs=1))
         work = ctx.enter_context(tc.tile_pool(name="work", bufs=8))
         psum = ctx.enter_context(tc.psum_pool(name="psum", bufs=8))
 
@@ -40,73 +41,77 @@ def tile_list_hwayt_dl_siluP_kernel(
         def picked(window, j0, j1):
             return window[:].indirect(offsets[:, j0 // PER_COL : j1 // PER_COL])
 
-        whd_raw = big.tile([P, PACK, N], F32, tag="big", name="whd_raw", align_bytes=64)
-        nc.sync.dma_start(whd_raw[:], whd.rearrange("(p i) n -> p i n", i=PACK))
+        def zero_other_rows(engines, tile):
+            for engine, (p0, p1) in zip(engines, ((0, ROW0), (32, 64), (64, P))):
+                engine.memset(tile[p0:p1, :].bitcast(I32), 0)
+
+        tabs = keep.tile([P, T], U8, name="tabs", align_bytes=64)
+        nc.sync.dma_start(tabs[ROW0 : ROW0 + 16, :].bitcast(I32), tab_scales[0].bitcast(I32))
+        s4_raw = keep.tile([P, 2 * N], U8, name="s4_raw", align_bytes=64)
+        for w, src in enumerate((wh4_scales, wg_scales)):
+            nc.sync.dma_start(s4_raw[ROW0 : ROW0 + 16, w * N : (w + 1) * N].bitcast(I32), src[0].bitcast(I32))
+        zero_other_rows((nc.gpsimd, nc.gpsimd, nc.gpsimd), s4_raw)
+        zero_other_rows((nc.vector, nc.vector, nc.gpsimd), tabs)
 
         w4_raw = [keep.tile([P, N], U16, name="w4_raw%d" % w, align_bytes=64) for w in range(2)]
         for w, src in enumerate((wh4_words, wg_words)):
             nc.sync.dma_start(w4_raw[w][:].bitcast(I32), src[0].bitcast(I32))
 
-        tabw = big.tile([P, T], U32, tag="big", name="tabw", align_bytes=64)
+        bias_raw = keep.tile([P, PACK], F32, name="bias_raw")
+        nc.sync.dma_start(bias_raw[:], bg.rearrange("(p i) -> p i", i=PACK))
+        whd_raw = big.tile([P, PACK, N], F32, tag="big1", name="whd_raw", align_bytes=64)
+        nc.sync.dma_start(whd_raw[:], whd.rearrange("(p i) n -> p i n", i=PACK))
+
+        tabw = big.tile([P, T], U32, tag="big2", name="tabw", align_bytes=64)
         nc.sync.dma_start(tabw[:].bitcast(I32), tab_words[0].rearrange("p t i -> p (t i)").bitcast(I32))
 
         r_rows = rT.rearrange("(p i) t -> p i t", i=PACK)
         r_tiles = []
 
         def load_r(i):
-            r_i = big.tile([P, T], F32, tag="big", name="r%d" % i, align_bytes=64)
+            r_i = big.tile([P, T], F32, tag="big%d" % (i % 3), name="r%d" % i, align_bytes=64)
             nc.sync.dma_start(r_i[:], r_rows[:, i, :])
             r_tiles.append(r_i)
 
-        load_r(0)
-
-        bias_raw = keep.tile([P, PACK], F32, name="bias_raw")
-        nc.scalar.dma_start(bias_raw[:], bg.rearrange("(p i) -> p i", i=PACK))
-
-        tabs = keep.tile([P, T], U8, name="tabs", align_bytes=64)
-        nc.vector.memset(tabs[:].bitcast(I32), 0)
-        nc.scalar.dma_start(tabs[0:P:8, :].bitcast(I32), tab_scales[0].bitcast(I32))
-
-        s4_raw = [keep.tile([P, N], U8, name="s4_raw%d" % w, align_bytes=64) for w in range(2)]
-        for w, src in enumerate((wh4_scales, wg_scales)):
-            nc.gpsimd.memset(s4_raw[w][:].bitcast(I32), 0)
-        for w, src in enumerate((wh4_scales, wg_scales)):
-            for q in range(4):
-                nc.gpsimd.dma_start(
-                    s4_raw[w][32 * q : 32 * q + 4, :].bitcast(I32), src[0, 4 * q : 4 * q + 4, :].bitcast(I32)
-                )
-
-        v_scales = keep.tile([P, J], U8, name="v_scales", align_bytes=64)
-        nc.vector.memset(v_scales[:].bitcast(I32), 0)
-        gathered_scales = keep.tile([P, J], U8, name="gathered_scales", align_bytes=64)
+        planes = keep.tile([P, J + 2 * N], U8, name="planes", align_bytes=64)
+        nc.gpsimd.memset(planes[:].bitcast(I32), 0)
+        staged = keep.tile([P, J + 2 * N], U8, name="staged", align_bytes=64)
+        nc.vector.tensor_copy(
+            staged[:, J:].rearrange("p (w i m) -> p w m i", w=2, i=PACK),
+            s4_raw[:].rearrange("p (w m i) -> p w m i", w=2, i=PACK),
+        )
+        gathered_scales = big.tile([P, J], U8, tag="big0", name="gathered_scales", align_bytes=64)
         nc.vector.tensor_copy(gathered_scales[:], picked(tabs, 0, J))
-        for r in range(4):
-            nc.scalar.dma_start(v_scales[r:P:32, :].bitcast(I32), gathered_scales[8 * r : P : 32, :].bitcast(I32))
+        nc.vector.tensor_copy(staged[:, 0:J].bitcast(I32), gathered_scales[:].bitcast(I32))
+        for q in range(4):
+            nc.sync.dma_start(
+                planes[32 * q : 32 * q + 4, :].bitcast(I32), staged[ROW0 + 4 * q : ROW0 + 4 * q + 4, :].bitcast(I32)
+            )
+        load_r(0)
+        v_scales = planes[:, 0:J]
+        s4 = [planes[:, J + w * N : J + (w + 1) * N] for w in range(2)]
+
+        w4 = [keep.tile([P, N], U16, name="w4_%d" % w, align_bytes=64) for w in range(2)]
+        for w in range(2):
+            nc.scalar.copy(
+                w4[w][:].rearrange("p (i m) -> p m i", i=PACK), w4_raw[w][:].rearrange("p (m i) -> p m i", i=PACK)
+            )
 
         half_bias = keep.tile([P, PACK], F32, name="half_bias")
         nc.vector.tensor_scalar_mul(half_bias[:], bias_raw[:], 0.5)
 
         whd_bf = keep.tile([P, PACK, P, PACK], BF16, name="whd_bf", align_bytes=64)
-        nc.scalar.copy(
-            whd_bf[:].rearrange("p i m e -> p m e i"),
-            whd_raw[:].rearrange("p e (m i) -> p m e i", i=PACK),
-        )
+        for m0 in range(0, P, P // 2):
+            nc.scalar.copy(
+                whd_bf[:, :, m0 : m0 + P // 2, :].rearrange("p i m e -> p m e i"),
+                whd_raw[:, :, PACK * m0 : PACK * (m0 + P // 2)].rearrange("p e (m i) -> p m e i", i=PACK),
+            )
         load_r(1)
         whd_codes = keep.tile([P, N], U32, name="whd_codes", align_bytes=64)
         whd_scales = keep.tile([P, N], U8, name="whd_scales", align_bytes=64)
         nc.vector.quantize_mx(
             out=whd_codes[:].bitcast(FP8X4), scales=whd_scales[:], in_=whd_bf[:].rearrange("p i m e -> p (i m e)")
         )
-
-        w4 = [keep.tile([P, N], U16, name="w4_%d" % w, align_bytes=64) for w in range(2)]
-        s4 = [keep.tile([P, N], U8, name="s4_%d" % w, align_bytes=64) for w in range(2)]
-        for w in range(2):
-            nc.scalar.copy(
-                w4[w][:].rearrange("p (i m) -> p m i", i=PACK), w4_raw[w][:].rearrange("p (m i) -> p m i", i=PACK)
-            )
-            nc.vector.tensor_copy(
-                s4[w][:].rearrange("p (i m) -> p m i", i=PACK), s4_raw[w][:].rearrange("p (m i) -> p m i", i=PACK)
-            )
 
         v_words = []
         for h in range(halves):

@@ -19,7 +19,8 @@ ALU = mybir.AluOpType
 P = 128
 PACK = 4
 HALF = 512
-CHUNK = 256
+QUARTER = 256
+LAST_EDGES = (0, 256, 512, 768, 896, 1024)
 PER_COL = 16
 ROW0 = 16
 
@@ -32,7 +33,7 @@ def tile_list_hwayt_dl_siluP_kernel(
     with ExitStack() as ctx:
         keep = ctx.enter_context(tc.tile_pool(name="keep", bufs=1))
         big = ctx.enter_context(tc.tile_pool(name="big", bufs=1))
-        work = ctx.enter_context(tc.tile_pool(name="work", bufs=8))
+        work = ctx.enter_context(tc.tile_pool(name="work", bufs=5))
         psum = ctx.enter_context(tc.psum_pool(name="psum", bufs=8))
 
         offsets = keep.tile([P, J // PER_COL], U16, name="offsets")
@@ -58,7 +59,6 @@ def tile_list_hwayt_dl_siluP_kernel(
             nc.sync.dma_start(w4_raw[w][:].bitcast(I32), src[0].bitcast(I32))
 
         bias_raw = keep.tile([P, PACK], F32, name="bias_raw")
-        nc.sync.dma_start(bias_raw[:], bg.rearrange("(p i) -> p i", i=PACK))
         whd_raw = big.tile([P, PACK, N], F32, tag="big1", name="whd_raw", align_bytes=64)
         nc.sync.dma_start(whd_raw[:], whd.rearrange("(p i) n -> p i n", i=PACK))
 
@@ -77,8 +77,8 @@ def tile_list_hwayt_dl_siluP_kernel(
         nc.gpsimd.memset(planes[:].bitcast(I32), 0)
         staged = keep.tile([P, J + 2 * N], U8, name="staged", align_bytes=64)
         nc.vector.tensor_copy(
-            staged[:, J:].rearrange("p (w i m) -> p w m i", w=2, i=PACK),
-            s4_raw[:].rearrange("p (w m i) -> p w m i", w=2, i=PACK),
+            staged[:, J:].rearrange("p (w i m) -> p w i m", w=2, i=PACK),
+            s4_raw[:].rearrange("p (w m i) -> p w i m", w=2, i=PACK),
         )
         gathered_scales = big.tile([P, J], U8, tag="big0", name="gathered_scales", align_bytes=64)
         nc.vector.tensor_copy(gathered_scales[:], picked(tabs, 0, J))
@@ -94,11 +94,12 @@ def tile_list_hwayt_dl_siluP_kernel(
         w4 = [keep.tile([P, N], U16, name="w4_%d" % w, align_bytes=64) for w in range(2)]
         for w in range(2):
             nc.scalar.copy(
-                w4[w][:].rearrange("p (i m) -> p m i", i=PACK), w4_raw[w][:].rearrange("p (m i) -> p m i", i=PACK)
+                w4[w][:].rearrange("p (i m) -> p i m", i=PACK), w4_raw[w][:].rearrange("p (m i) -> p i m", i=PACK)
             )
 
         half_bias = keep.tile([P, PACK], F32, name="half_bias")
-        nc.vector.tensor_scalar_mul(half_bias[:], bias_raw[:], 0.5)
+        nc.gpsimd.dma_start(bias_raw[:], bg.rearrange("(p i) -> p i", i=PACK))
+        nc.gpsimd.tensor_scalar(half_bias[:], bias_raw[:], 0.5, 0.0, ALU.mult, ALU.add)
 
         whd_bf = keep.tile([P, PACK, P, PACK], BF16, name="whd_bf", align_bytes=64)
         for m0 in range(0, P, P // 2):
@@ -116,7 +117,10 @@ def tile_list_hwayt_dl_siluP_kernel(
         v_words = []
         for h in range(halves):
             words_h = keep.tile([P, HALF], U32, name="v_words%d" % h, align_bytes=64)
-            nc.vector.tensor_copy(words_h[:], picked(tabw, h * HALF, (h + 1) * HALF))
+            for o in range(0, HALF, QUARTER):
+                nc.vector.tensor_copy(
+                    words_h[:, o : o + QUARTER], picked(tabw, h * HALF + o, h * HALF + o + QUARTER)
+                )
             v_words.append(words_h)
         load_r(2)
 
@@ -127,53 +131,69 @@ def tile_list_hwayt_dl_siluP_kernel(
         out_rows = out_0.rearrange("(p i) j -> p i j", i=PACK)
         out_words = out_1[0].rearrange("p j i -> p (j i)").bitcast(I32)
 
-        for i in range(PACK):
+        y_bf3 = y_bf[:].rearrange("p (j i) -> p j i", i=PACK)
+
+        def round_pair(i0, j0, j1):
+            nc.scalar.copy(y_bf3[:, j0:j1, i0 : i0 + 2], y[:, i0 : i0 + 2, j0:j1].rearrange("p i j -> p j i"))
+
+        half_cols = [slice(h * HALF, (h + 1) * HALF) for h in range(halves)]
+        last = PACK - 1
+
+        def products(i, width):
             cols = slice(i * P, (i + 1) * P)
-            made, keep_share = [], []
-            for h in range(halves):
-                js = slice(h * HALF, (h + 1) * HALF)
-                rhs = v_words[h][:].bitcast(FP8X4)
-                ha = psum.tile([P, HALF], F32, tag="acc", name="ha")
+            silu = work.tile([P, J], F32, name="silu")
+            tanh = work.tile([P, J], F32, name="tanh")
+            for j0 in range(0, J, width):
+                js = slice(j0, j0 + width)
+                h, o = divmod(j0, HALF)
+                rhs = v_words[h][:, o : o + width].bitcast(FP8X4)
+                ha = psum.tile([P, width], F32, tag="acc", name="ha")
                 nc.tensor.matmul_mx(ha[:], w4[0][:, cols].bitcast(FP4X4), s4[0][:, cols], rhs, v_scales[:, js],
                                     start=True, stop=False)
                 nc.tensor.matmul_mx(ha[:], whd_codes[:, cols].bitcast(FP8X4), whd_scales[:, cols], rhs,
                                     v_scales[:, js], start=False, stop=True)
-                ga = psum.tile([P, HALF], F32, tag="acc", name="ga")
+                ga = psum.tile([P, width], F32, tag="acc", name="ga")
                 nc.tensor.matmul_mx(ga[:], w4[1][:, cols].bitcast(FP4X4), s4[1][:, cols], rhs, v_scales[:, js],
                                     start=True, stop=True)
-                s = work.tile([P, HALF], F32, name="s")
-                nc.scalar.activation(s[:], ha[:], ACT.Silu)
-                th = work.tile([P, HALF], F32, name="th")
-                nc.scalar.activation(th[:], ga[:], ACT.Tanh, bias=half_bias[:, i : i + 1], scale=0.5)
-                u = work.tile([P, HALF], F32, name="u")
-                nc.scalar.activation(u[:], th[:], ACT.Copy, bias=0.5, scale=-0.5)
-                gs2 = work.tile([P, HALF], F32, name="gs2")
-                nc.vector.scalar_tensor_tensor(gs2[:], th[:], 1.0, s[:], ALU.add, ALU.mult)
-                made.append(gs2)
-                keep_share.append(u)
-            step = HALF if i < PACK - 1 else CHUNK
-            for j0 in range(0, J, step):
-                h, o = divmod(j0, HALF)
-                ru = work.tile([P, step], F32, name="ru")
-                nc.vector.tensor_tensor(ru[:], picked(r_tiles[i], j0, j0 + step), keep_share[h][:, o : o + step], ALU.mult)
-                nc.vector.scalar_tensor_tensor(
-                    y[:, i, j0 : j0 + step], made[h][:, o : o + step], 0.5, ru[:], ALU.mult, ALU.add
-                )
-                if i == PACK - 1:
-                    nc.sync.dma_start(out_rows[:, i, j0 : j0 + step], y[:, i, j0 : j0 + step])
-                    bf = y_bf[:, PACK * j0 : PACK * (j0 + step)]
-                    nc.scalar.copy(
-                        bf.rearrange("p (c a i) -> p c i a", a=4, i=PACK),
-                        y[:, :, j0 : j0 + step].rearrange("p i (c a) -> p c i a", a=4),
-                    )
-                    nc.vector.quantize_mx(
-                        out=y_codes[:, j0 : j0 + step].bitcast(FP8X4), scales=y_scales[:, j0 : j0 + step], in_=bf
-                    )
-                    nc.sync.dma_start(out_words[:, j0 : j0 + step], y_codes[:, j0 : j0 + step].bitcast(I32))
+                nc.scalar.activation(silu[:, js], ha[:], ACT.Silu)
+                nc.scalar.activation(tanh[:, js], ga[:], ACT.Tanh, bias=half_bias[:, i : i + 1], scale=0.5)
+            return silu, tanh
+
+        silu, tanh = products(0, QUARTER)
+        carry = keep.tile([P, J], F32, tag="share0", name="carry")
+        made = keep.tile([P, J], F32, name="made")
+        for j0 in range(0, J, QUARTER):
+            js = slice(j0, j0 + QUARTER)
+            nc.vector.tensor_scalar(carry[:, js], tanh[:, js], -0.5, 0.5, ALU.mult, ALU.add)
+            nc.vector.scalar_tensor_tensor(made[:, js], tanh[:, js], 1.0, silu[:, js], ALU.add, ALU.mult)
+
+        for i in range(last):
+            kept = work.tile([P, J], F32, name="kept")
+            nc.vector.tensor_tensor(kept[:], picked(r_tiles[i], 0, J), carry[:], ALU.mult)
             if i == 0:
-                load_r(3)
-            if i < PACK - 1:
-                nc.sync.dma_start(out_rows[:, i, :], y[:, i, :])
+                load_r(last)
+            silu, tanh = products(i + 1, HALF)
+            carry = keep.tile([P, J], F32, tag="share%d" % (i + 1), name="carry")
+            nc.scalar.activation(carry[:], tanh[:], ACT.Copy, bias=0.5, scale=-0.5)
+            made_next = keep.tile([P, J], F32, tag="share%d" % i, name="made_next")
+            nc.vector.scalar_tensor_tensor(made_next[:], tanh[:], 1.0, silu[:], ALU.add, ALU.mult)
+            nc.vector.scalar_tensor_tensor(y[:, i, :], made[:], 0.5, kept[:], ALU.mult, ALU.add)
+            nc.sync.dma_start(out_rows[:, i, :], y[:, i, :])
+            made = made_next
+
+        for js in half_cols:
+            round_pair(0, js.start, js.stop)
+        for j0, j1 in zip(LAST_EDGES, LAST_EDGES[1:]):
+            kept = work.tile([P, j1 - j0], F32, name="kept_piece")
+            nc.vector.tensor_tensor(kept[:], picked(r_tiles[last], j0, j1), carry[:, j0:j1], ALU.mult)
+            nc.vector.scalar_tensor_tensor(y[:, last, j0:j1], made[:, j0:j1], 0.5, kept[:], ALU.mult, ALU.add)
+            if j1 % HALF == 0:
+                nc.sync.dma_start(out_rows[:, last, j1 - HALF : j1], y[:, last, j1 - HALF : j1])
+            round_pair(2, j0, j1)
+            nc.vector.quantize_mx(
+                out=y_codes[:, j0:j1].bitcast(FP8X4), scales=y_scales[:, j0:j1], in_=y_bf[:, PACK * j0 : PACK * j1]
+            )
+            nc.sync.dma_start(out_words[:, j0:j1], y_codes[:, j0:j1].bitcast(I32))
         for q in range(4):
             eng = nc.scalar if q % 2 else nc.sync
             eng.dma_start(out_2[0, 4 * q : 4 * q + 4, :].bitcast(I32), y_scales[32 * q : 32 * q + 4, :].bitcast(I32))

from contextlib import ExitStack

import concourse.mybir as mybir

K, N, T, J = 512, 512, 4096, 1024
FLOPS = 3 * 2 * K * N * J

F32 = mybir.dt.float32
BF16 = mybir.dt.bfloat16
I32 = mybir.dt.int32
U32 = mybir.dt.uint32
U16 = mybir.dt.uint16
U8 = mybir.dt.uint8
FP8X4 = mybir.dt.float8_e4m3fn_x4
FP4X4 = mybir.dt.float4_e2m1fn_x4
ACT = mybir.ActivationFunctionType
ALU = mybir.AluOpType

P = 128
PACK = 4
HALF = 512
QUARTER = 256
LAST_EDGES = (0, 256, 512, 768, 896, 1024)
PER_COL = 16
ROW0 = 16


def tile_list_hwayt_dl_siluP_kernel(
    tc, tab_words, tab_scales, wg_words, wg_scales, wh4_words, wh4_scales, whd, bg, rT, offs, out_0, out_1, out_2
):
    nc = tc.nc
    halves = J // HALF
    with ExitStack() as ctx:
        keep = ctx.enter_context(tc.tile_pool(name="keep", bufs=1))
        big = ctx.enter_context(tc.tile_pool(name="big", bufs=1))
        work = ctx.enter_context(tc.tile_pool(name="work", bufs=5))
        psum = ctx.enter_context(tc.psum_pool(name="psum", bufs=8))

        offsets = keep.tile([P, J // PER_COL], U16, name="offsets")
        nc.sync.dma_start(offsets[:], offs)

        def picked(window, j0, j1):
            return window[:].indirect(offsets[:, j0 // PER_COL : j1 // PER_COL])

        def zero_other_rows(engines, tile):
            for engine, (p0, p1) in zip(engines, ((0, ROW0), (32, 64), (64, P))):
                engine.memset(tile[p0:p1, :].bitcast(I32), 0)

        tabs = keep.tile([P, T], U8, name="tabs", align_bytes=64)
        nc.sync.dma_start(tabs[ROW0 : ROW0 + 16, :].bitcast(I32), tab_scales[0].bitcast(I32))
        s4_raw = keep.tile([P, 2 * N], U8, name="s4_raw", align_bytes=64)
        for w, src in enumerate((wh4_scales, wg_scales)):
            nc.sync.dma_start(s4_raw[ROW0 : ROW0 + 16, w * N : (w + 1) * N].bitcast(I32), src[0].bitcast(I32))
        zero_other_rows((nc.gpsimd, nc.gpsimd, nc.gpsimd), s4_raw)
        zero_other_rows((nc.vector, nc.vector, nc.gpsimd), tabs)

        w4_raw = [keep.tile([P, N], U16, name="w4_raw%d" % w, align_bytes=64) for w in range(2)]
        for w, src in enumerate((wh4_words, wg_words)):
            nc.sync.dma_start(w4_raw[w][:].bitcast(I32), src[0].bitcast(I32))

        bias_raw = keep.tile([P, PACK], F32, name="bias_raw")
        whd_raw = big.tile([P, PACK, N], F32, tag="big1", name="whd_raw", align_bytes=64)
        nc.sync.dma_start(whd_raw[:], whd.rearrange("(p i) n -> p i n", i=PACK))

        tabw = big.tile([P, T], U32, tag="big2", name="tabw", align_bytes=64)
        nc.sync.dma_start(tabw[:].bitcast(I32), tab_words[0].rearrange("p t i -> p (t i)").bitcast(I32))

        r_rows = rT.rearrange("(p i) t -> p i t", i=PACK)
        r_tiles = []

        def load_r(i):
            r_i = big.tile([P, T], F32, tag="big%d" % (i % 3), name="r%d" % i, align_bytes=64)
            nc.sync.dma_start(r_i[:], r_rows[:, i, :])
            r_tiles.append(r_i)

        planes = keep.tile([P, J + 2 * N], U8, name="planes", align_bytes=64)
        nc.gpsimd.memset(planes[:].bitcast(I32), 0)
        staged = keep.tile([P, J + 2 * N], U8, name="staged", align_bytes=64)
        nc.vector.tensor_copy(
            staged[:, J:].rearrange("p (w i m) -> p w i m", w=2, i=PACK),
            s4_raw[:].rearrange("p (w m i) -> p w i m", w=2, i=PACK),
        )
        gathered_scales = big.tile([P, J], U8, tag="big0", name="gathered_scales", align_bytes=64)
        nc.vector.tensor_copy(gathered_scales[:], picked(tabs, 0, J))
        nc.vector.tensor_copy(staged[:, 0:J].bitcast(I32), gathered_scales[:].bitcast(I32))
        for q in range(4):
            nc.sync.dma_start(
                planes[32 * q : 32 * q + 4, :].bitcast(I32), staged[ROW0 + 4 * q : ROW0 + 4 * q + 4, :].bitcast(I32)
            )
        load_r(0)
        v_scales = planes[:, 0:J]
        s4 = [planes[:, J + w * N : J + (w + 1) * N] for w in range(2)]

        w4 = [keep.tile([P, N], U16, name="w4_%d" % w, align_bytes=64) for w in range(2)]
        for w in range(2):
            nc.scalar.copy(
                w4[w][:].rearrange("p (i m) -> p i m", i=PACK), w4_raw[w][:].rearrange("p (m i) -> p i m", i=PACK)
            )

        half_bias = keep.tile([P, PACK], F32, name="half_bias")
        nc.gpsimd.dma_start(bias_raw[:], bg.rearrange("(p i) -> p i", i=PACK))
        nc.gpsimd.tensor_scalar(half_bias[:], bias_raw[:], 0.5, 0.0, ALU.mult, ALU.add)

        whd_bf = keep.tile([P, PACK, P, PACK], BF16, name="whd_bf", align_bytes=64)
        for m0 in range(0, P, P // 2):
            nc.scalar.copy(
                whd_bf[:, :, m0 : m0 + P // 2, :].rearrange("p i m e -> p m e i"),
                whd_raw[:, :, PACK * m0 : PACK * (m0 + P // 2)].rearrange("p e (m i) -> p m e i", i=PACK),
            )
        load_r(1)
        whd_codes = keep.tile([P, N], U32, name="whd_codes", align_bytes=64)
        whd_scales = keep.tile([P, N], U8, name="whd_scales", align_bytes=64)
        nc.vector.quantize_mx(
            out=whd_codes[:].bitcast(FP8X4), scales=whd_scales[:], in_=whd_bf[:].rearrange("p i m e -> p (i m e)")
        )

        v_words = []
        for h in range(halves):
            words_h = keep.tile([P, HALF], U32, name="v_words%d" % h, align_bytes=64)
            for o in range(0, HALF, QUARTER):
                nc.vector.tensor_copy(
                    words_h[:, o : o + QUARTER], picked(tabw, h * HALF + o, h * HALF + o + QUARTER)
                )
            v_words.append(words_h)
        load_r(2)

        y = keep.tile([P, PACK, J], F32, name="y", align_bytes=64)
        y_bf = keep.tile([P, J * PACK], BF16, name="y_bf", align_bytes=64)
        y_codes = keep.tile([P, J], U32, name="y_codes", align_bytes=64)
        y_scales = keep.tile([P, J], U8, name="y_scales", align_bytes=64)
        out_rows = out_0.rearrange("(p i) j -> p i j", i=PACK)
        out_words = out_1[0].rearrange("p j i -> p (j i)").bitcast(I32)

        y_bf3 = y_bf[:].rearrange("p (j i) -> p j i", i=PACK)

        def round_pair(i0, j0, j1):
            nc.scalar.copy(y_bf3[:, j0:j1, i0 : i0 + 2], y[:, i0 : i0 + 2, j0:j1].rearrange("p i j -> p j i"))

        half_cols = [slice(h * HALF, (h + 1) * HALF) for h in range(halves)]
        last = PACK - 1

        def products(i, width):
            cols = slice(i * P, (i + 1) * P)
            silu = work.tile([P, J], F32, name="silu")
            tanh = work.tile([P, J], F32, name="tanh")
            for j0 in range(0, J, width):
                js = slice(j0, j0 + width)
                h, o = divmod(j0, HALF)
                rhs = v_words[h][:, o : o + width].bitcast(FP8X4)
                ha = psum.tile([P, width], F32, tag="acc", name="ha")
                nc.tensor.matmul_mx(ha[:], w4[0][:, cols].bitcast(FP4X4), s4[0][:, cols], rhs, v_scales[:, js],
                                    start=True, stop=False)
                nc.tensor.matmul_mx(ha[:], whd_codes[:, cols].bitcast(FP8X4), whd_scales[:, cols], rhs,
                                    v_scales[:, js], start=False, stop=True)
                ga = psum.tile([P, width], F32, tag="acc", name="ga")
                nc.tensor.matmul_mx(ga[:], w4[1][:, cols].bitcast(FP4X4), s4[1][:, cols], rhs, v_scales[:, js],
                                    start=True, stop=True)
                nc.scalar.activation(silu[:, js], ha[:], ACT.Silu)
                nc.scalar.activation(tanh[:, js], ga[:], ACT.Tanh, bias=half_bias[:, i : i + 1], scale=0.5)
            return silu, tanh

        silu, tanh = products(0, QUARTER)
        carry = keep.tile([P, J], F32, tag="share0", name="carry")
        made = keep.tile([P, J], F32, name="made")
        for j0 in range(0, J, QUARTER):
            js = slice(j0, j0 + QUARTER)
            nc.vector.tensor_scalar(carry[:, js], tanh[:, js], -0.5, 0.5, ALU.mult, ALU.add)
            nc.vector.scalar_tensor_tensor(made[:, js], tanh[:, js], 1.0, silu[:, js], ALU.add, ALU.mult)

        for i in range(last):
            kept = work.tile([P, J], F32, name="kept")
            nc.vector.tensor_tensor(kept[:], picked(r_tiles[i], 0, J), carry[:], ALU.mult)
            if i == 0:
                load_r(last)
            silu, tanh = products(i + 1, HALF)
            carry = keep.tile([P, J], F32, tag="share%d" % (i + 1), name="carry")
            nc.scalar.activation(carry[:], tanh[:], ACT.Copy, bias=0.5, scale=-0.5)
            made_next = keep.tile([P, J], F32, tag="share%d" % i, name="made_next")
            nc.vector.scalar_tensor_tensor(made_next[:], tanh[:], 1.0, silu[:], ALU.add, ALU.mult)
            nc.vector.scalar_tensor_tensor(y[:, i, :], made[:], 0.5, kept[:], ALU.mult, ALU.add)
            nc.sync.dma_start(out_rows[:, i, :], y[:, i, :])
            made = made_next

        for js in half_cols:
            round_pair(0, js.start, js.stop)
        for j0, j1 in zip(LAST_EDGES, LAST_EDGES[1:]):
            kept = work.tile([P, j1 - j0], F32, name="kept_piece")
            nc.vector.tensor_tensor(kept[:], picked(r_tiles[last], j0, j1), carry[:, j0:j1], ALU.mult)
            nc.vector.scalar_tensor_tensor(y[:, last, j0:j1], made[:, j0:j1], 0.5, kept[:], ALU.mult, ALU.add)
            if j1 % HALF == 0:
                nc.sync.dma_start(out_rows[:, last, j1 - HALF : j1], y[:, last, j1 - HALF : j1])
            round_pair(2, j0, j1)
            nc.vector.quantize_mx(
                out=y_codes[:, j0:j1].bitcast(FP8X4), scales=y_scales[:, j0:j1], in_=y_bf[:, PACK * j0 : PACK * j1]
            )
            nc.sync.dma_start(out_words[:, j0:j1], y_codes[:, j0:j1].bitcast(I32))
        for q in range(4):
            eng = nc.scalar if q % 2 else nc.sync
            eng.dma_start(out_2[0, 4 * q : 4 * q + 4, :].bitcast(I32), y_scales[32 * q : 32 * q + 4, :].bitcast(I32))
